import numpy as np
import ml_dtypes


def mxq(x, axis, fmt="e4m3"):
    dtype, down = {"e4m3": (ml_dtypes.float8_e4m3fn, 7), "e5m2": (ml_dtypes.float8_e5m2, 14)}[fmt]
    v = np.moveaxis(np.asarray(x, np.float32).astype(ml_dtypes.bfloat16).astype(np.float64), axis, -1)
    blocks = v.reshape(v.shape[:-1] + (-1, 32))
    amax = np.abs(blocks).max(-1, keepdims=True)
    byte = np.maximum(np.where(amax > 0, np.frexp(amax)[1] - 1 + 127, 0) - down, 1)
    scale = np.exp2(byte - 127.0)
    codes = (blocks / scale).astype(np.float32).astype(dtype).astype(np.float64)
    return np.moveaxis((codes * scale).reshape(v.shape), -1, axis)


WIDE = False


def mx_kscale(k, group=512):
    if not WIDE:
        return np.ones(k)
    levels = np.array([10, -10, 5, -5, 0])
    if group != 512:
        return np.exp2(np.random.permutation(np.resize(levels, k // group))).repeat(group)
    if k % 512:
        return np.exp2(np.random.permutation(np.resize(levels, k // 32))).repeat(32)
    a = np.empty((k // 512, 16))
    for p in range(k // 512):
        a[p, :8] = np.random.permutation(np.resize(levels, 8))
        for g in range(8):
            far = levels[np.abs(levels - a[p, g]) >= 10]
            a[p, g + 8] = far[np.random.randint(len(far))]
    return np.exp2(a.ravel()).repeat(32)


def f64(x):
    return np.asarray(x).astype(np.float64)


E2M1 = np.array([0.0, 0.5, 1.0, 1.5, 2.0, 3.0, 4.0, 6.0, -0.0, -0.5, -1.0, -1.5, -2.0, -3.0, -4.0, -6.0])


def pack_group(w):
    k, n = w.shape
    w = f64(np.asarray(w, np.float32).astype(ml_dtypes.bfloat16)).reshape(k // 32, 32, n)
    amax = np.abs(w).max(1)
    mant, ex = np.frexp(amax / 6.0)
    byte = np.clip(np.where(amax > 0, np.where(mant > 0.5, ex, ex - 1) + 127, 1), 1, 254)
    scaled = (w * np.exp2(127.0 - byte)[:, None, :]).reshape(k, n).astype(np.float32)
    c = np.ascontiguousarray(scaled.reshape(k // 4, 4, n).transpose(0, 2, 1)).astype(ml_dtypes.float4_e2m1fn).view(np.uint8) & 0xF
    return np.ascontiguousarray((c[..., 0::2] | (c[..., 1::2] << 4)).reshape(k // 4, 2 * n)), byte.astype(np.uint8)


def unpack_group(words, scales):
    p, n = words.shape[0], scales.shape[1]
    words = np.ascontiguousarray(words).reshape(p, n, 2)
    nib = np.empty((p, n, 4), np.uint8)
    nib[..., 0::2] = words & 0xF
    nib[..., 1::2] = words >> 4
    return E2M1[nib].transpose(0, 2, 1).reshape(4 * p, n) * np.repeat(np.exp2(scales.astype(np.float64) - 127.0), 32, axis=0)


def sigmoid(v):
    return 1.0 / (1.0 + np.exp(-v))


G, D, M, O, N = 2, 256, 256, 256, 512


def setup_inputs():
    n = np.random.standard_normal
    s_d = mx_kscale(D, 0)
    s_o = mx_kscale(O, 0)
    w1_ = [pack_group(w) for w in n((G, D, M)) / np.sqrt(D) / s_d[:, None]]
    w2_ = [pack_group(w) for w in n((G, D, M)) / np.sqrt(D) / s_d[:, None]]
    wo_ = [pack_group(w) for w in n((G, O, M)) / np.sqrt(O) / s_o[:, None]]
    return {
        "x": (n((G, D, N)) * s_d[:, None]).astype(np.float32),
        "w1_words": np.stack([w[0] for w in w1_]),
        "w1_scales": np.stack([w[1] for w in w1_]),
        "w2_words": np.stack([w[0] for w in w2_]),
        "w2_scales": np.stack([w[1] for w in w2_]),
        "th": (np.random.uniform(0.5, 1.5, (G, M, 1))).astype(np.float32),
        "wo_words": np.stack([w[0] for w in wo_]),
        "wo_scales": np.stack([w[1] for w in wo_]),
        "dy": (n((G, O, N)) * s_o[:, None]).astype(np.float32),
        "old": (0.3 * n((G, M, N))).astype(np.float32),
    }


def reference(x, w1_words, w1_scales, w2_words, w2_scales, th, wo_words, wo_scales, dy, old):
    w1 = np.stack([unpack_group(w1_words[g], w1_scales[g]) for g in range(G)])
    xq = mxq(f64(x), 1, "e4m3")
    z1 = w1.transpose(0, 2, 1) @ xq
    w2 = np.stack([unpack_group(w2_words[g], w2_scales[g]) for g in range(G)])
    z2 = w2.transpose(0, 2, 1) @ xq
    mg = np.sqrt(np.square(z1) + np.square(z2) + 0.05)
    wo = np.stack([unpack_group(wo_words[g], wo_scales[g]) for g in range(G)])
    dyq = mxq(f64(dy), 1, "e4m3")
    c0 = wo.transpose(0, 2, 1) @ dyq
    dmg = c0 * sigmoid(mg - f64(th)) + c0 * mg * sigmoid(mg - f64(th)) * (1.0 - sigmoid(mg - f64(th)))
    dz1 = dmg * 0.5 / np.sqrt(np.square(z1) + np.square(z2) + 0.05) * z1 * 2.0
    y = dz1 + f64(old)
    return y

@@ -1,0 +1,183 @@
+from contextlib import ExitStack
+
+import concourse.mybir as mybir
+
+G, D, M, N = 2, 256, 256, 512
+FLOPS = 3 * 2 * G * D * M * N
+
+F32 = mybir.dt.float32
+BF16 = mybir.dt.bfloat16
+I32 = mybir.dt.int32
+U32 = mybir.dt.uint32
+U8 = mybir.dt.uint8
+FP8X4 = mybir.dt.float8_e4m3fn_x4
+FP4X4 = mybir.dt.float4_e2m1fn_x4
+ACT = mybir.ActivationFunctionType
+ALU = mybir.AluOpType
+
+P = 128
+PACK = 4
+ROWS = D // PACK
+TILES = G * M // P
+FLOOR = 0.05
+X_SPLIT = 336
+MG_SPLIT = 256
+
+
+def tile_rows_bmagnitude_kernel(tc, x, w1_words, w1_scales, w2_words, w2_scales, th, wo_words, wo_scales, dy, old, out):
+    nc = tc.nc
+    with ExitStack() as ctx:
+        sb = ctx.enter_context(tc.tile_pool(name="sb", bufs=1))
+        ps = ctx.enter_context(tc.psum_pool(name="ps", bufs=1))
+        ctx.enter_context(tc.manual_schedule())
+
+        def group(t):
+            return t % G
+
+        def half(t):
+            return t // G
+
+        def load_rows(name, src):
+            raw = sb.tile([P, PACK, N], F32, name=name)
+            nc.sync.dma_start(out=raw[:], in_=src.rearrange("g (p j) n -> (g p) j n", j=PACK))
+            return raw
+
+        def load_words(name, words):
+            w = sb.tile([P, 2 * M], U8, name=name, align_bytes=64)
+            nc.sync.dma_start(out=w[:].bitcast(I32), in_=words.rearrange("g p b -> (g p) b").bitcast(I32))
+            return w
+
+        planes = sb.tile([P, 3, M], U8, name="planes", align_bytes=64)
+        nc.vector.memset(planes[:].rearrange("p i m -> p (i m)").bitcast(I32), 0)
+
+        def load_scales(queue, i, scales):
+            rows = scales.rearrange("g f m -> (g f) m").bitcast(I32)
+            for q in range(4):
+                queue.dma_start(out=planes[32 * q:32 * q + 4, i, :].bitcast(I32), in_=rows[4 * q:4 * q + 4, :])
+            return planes[:, i, :]
+
+        x_raw = load_rows("x_raw", x)
+        w1 = (load_words("w1", w1_words), load_scales(nc.scalar, 0, w1_scales))
+        w2 = (load_words("w2", w2_words), load_scales(nc.gpsimd, 1, w2_scales))
+        dy_raw = load_rows("dy_raw", dy)
+        wo = (load_words("wo", wo_words), load_scales(nc.sync, 2, wo_scales))
+        th_sb = sb.tile([P, G, M // P], F32, name="th_sb")
+        with nc.allow_non_contiguous_dma(reason="one threshold a partition"):
+            nc.sync.dma_start(out=th_sb[:], in_=th.rearrange("g (h p) o -> p g (h o)", p=P))
+        old_sb = sb.tile([P, G * (M // P), N], F32, name="old_sb")
+        nc.sync.dma_start(out=old_sb[:], in_=old.rearrange("g (h p) n -> p (g h) n", p=P))
+
+        warm = sb.tile([P, 8], F32, name="warm")
+        nc.vector.memset(warm[:, 0:1], 1.0)
+        warm_out = sb.tile([P, 8], F32, name="warm_out")
+        nc.scalar.activation(out=warm_out[:, 0:1], in_=warm[:, 0:1], func=ACT.Abs_reciprocal_sqrt)
+
+        def interleave(copy, grouped, raw, lo, hi):
+            copy(out=grouped[:, lo:hi, :].rearrange("p (c i) j -> p c j i", i=4),
+                 in_=raw[:, :, lo:hi].rearrange("p j (c i) -> p c j i", i=4))
+
+        def quantize(name, grouped):
+            codes = sb.tile([P, N], U32, name=name + "_codes", align_bytes=64)
+            scales = sb.tile([P, N], U8, name=name + "_scales", align_bytes=64)
+            nc.vector.quantize_mx(out=codes[:].bitcast(FP8X4), scales=scales[:], in_=grouped[:].rearrange("p n j -> p (n j)"))
+            return codes, scales
+
+        def product(bank, weights, moving, t):
+            rows = slice(ROWS * group(t), ROWS * (group(t) + 1))
+            w, ws = weights
+            codes, scales = moving
+            nc.tensor.matmul_mx(
+                out=bank[:],
+                lhsT=w[rows, 2 * P * half(t):2 * P * (half(t) + 1)].bitcast(FP4X4),
+                lhsT_scale=ws[rows, P * half(t):P * (half(t) + 1)],
+                rhs=codes[rows, :].bitcast(FP8X4),
+                rhs_scale=scales[rows, :],
+                start=True,
+                stop=True,
+            )
+
+        def tiles(name):
+            return [sb.tile([P, N], F32, name="%s%d" % (name, t)) for t in range(TILES)]
+
+        x_grouped = sb.tile([P, N, PACK], BF16, name="x_grouped", align_bytes=64)
+        interleave(nc.vector.tensor_copy, x_grouped, x_raw, 0, X_SPLIT)
+        interleave(nc.scalar.copy, x_grouped, x_raw, X_SPLIT, N)
+        xq = quantize("x", x_grouped)
+
+        z1 = [ps.tile([P, N], F32, name="z1_%d" % t) for t in range(TILES)]
+        zc = [ps.tile([P, N], F32, name="zc_%d" % t) for t in range(TILES)]
+        for t in range(TILES):
+            product(z1[t], w1, xq, t)
+            product(zc[t], w2, xq, t)
+
+        sq1, sq2, ss, rs, mg = tiles("sq1_"), tiles("sq2_"), tiles("ss"), tiles("rs"), tiles("mg")
+        cosine, pre, sig = tiles("cosine"), tiles("pre"), tiles("sig")
+        h, k, m, res = tiles("h"), tiles("k"), tiles("m"), tiles("res")
+
+        def squares(t):
+            nc.scalar.activation(out=sq1[t][:], in_=z1[t][:], func=ACT.Square)
+            nc.scalar.activation(out=sq2[t][:], in_=zc[t][:], func=ACT.Square)
+
+        def add(t):
+            nc.vector.scalar_tensor_tensor(out=ss[t][:], in0=sq1[t][:], scalar=FLOOR, in1=sq2[t][:], op0=ALU.add, op1=ALU.add)
+
+        def root(t):
+            nc.scalar.activation(out=rs[t][:], in_=ss[t][:], func=ACT.Abs_reciprocal_sqrt)
+
+        def magnitude(eng, t, lo, hi):
+            eng.tensor_tensor(out=mg[t][:, lo:hi], in0=ss[t][:, lo:hi], in1=rs[t][:, lo:hi], op=ALU.mult)
+
+        def step_e(t):
+            nc.vector.tensor_tensor(out=cosine[t][:], in0=rs[t][:], in1=z1[t][:], op=ALU.mult)
+
+        def step_f(t):
+            nc.vector.tensor_tensor(out=pre[t][:], in0=cosine[t][:], in1=zc[t][:], op=ALU.mult)
+
+        dy_grouped = sb.tile([P, N, PACK], BF16, name="dy_grouped", align_bytes=64)
+        neg_th = sb.tile([P, G, M // P], F32, name="neg_th")
+
+        squares(0)
+        interleave(nc.vector.tensor_copy, dy_grouped, dy_raw, 0, N)
+        add(0)
+        squares(1)
+        dyq = quantize("dy", dy_grouped)
+        product(zc[0], wo, dyq, 0)
+        product(zc[1], wo, dyq, 1)
+        add(1)
+        root(0)
+        magnitude(nc.gpsimd, 0, 0, N)
+        step_e(0)
+        nc.vector.tensor_scalar(out=neg_th[:], in0=th_sb[:], scalar1=-1.0, scalar2=None, op0=ALU.mult)
+        step_f(0)
+        squares(2)
+        product(zc[2], wo, dyq, 2)
+        add(2)
+        squares(3)
+        product(zc[3], wo, dyq, 3)
+        add(3)
+        for t in range(1, TILES):
+            root(t)
+        magnitude(nc.gpsimd, 1, 0, N)
+        magnitude(nc.gpsimd, 2, 0, N)
+        magnitude(nc.gpsimd, 3, 0, MG_SPLIT)
+        step_e(1)
+        step_e(2)
+        step_f(1)
+        step_e(3)
+        step_f(2)
+        step_f(3)
+        magnitude(nc.vector, 3, MG_SPLIT, N)
+
+        for t in range(TILES):
+            nc.scalar.activation(out=sig[t][:], in_=mg[t][:], func=ACT.Sigmoid, bias=neg_th[:, group(t), half(t):half(t) + 1])
+
+        for pair in range(0, TILES, 2):
+            for t in (pair, pair + 1):
+                nc.vector.scalar_tensor_tensor(out=h[t][:], in0=sig[t][:], scalar=1.0, in1=mg[t][:], op0=ALU.subtract, op1=ALU.mult)
+            for t in (pair, pair + 1):
+                nc.vector.scalar_tensor_tensor(out=k[t][:], in0=h[t][:], scalar=1.0, in1=sig[t][:], op0=ALU.subtract, op1=ALU.mult)
+            for t in (pair, pair + 1):
+                nc.vector.tensor_tensor(out=m[t][:], in0=k[t][:], in1=pre[t][:], op=ALU.mult)
+            for t in (pair, pair + 1):
+                nc.vector.tensor_tensor(out=res[t][:], in0=old_sb[:, (M // P) * group(t) + half(t), :], in1=m[t][:], op=ALU.subtract)
+                nc.sync.dma_start(out=out[group(t), P * half(t):P * (half(t) + 1), :], in_=res[t][:])

@@ -32,10 +32,10 @@ def tile_rows_bmagnitude_kernel(tc, x, w1_words, w1_scales, w2_words, w2_scales,
         ctx.enter_context(tc.manual_schedule())
 
         def group(t):
-            return t % G
+            return t // 2
 
         def half(t):
-            return t // G
+            return t % 2
 
         def load_rows(name, src):
             raw = sb.tile([P, PACK, N], F32, name=name)
@@ -50,17 +50,22 @@ def tile_rows_bmagnitude_kernel(tc, x, w1_words, w1_scales, w2_words, w2_scales,
         planes = sb.tile([P, 3, M], U8, name="planes", align_bytes=64)
         nc.vector.memset(planes[:].rearrange("p i m -> p (i m)").bitcast(I32), 0)
 
-        def load_scales(queue, i, scales):
+        def load_scales(i, scales, g):
             rows = scales.rearrange("g f m -> (g f) m").bitcast(I32)
-            for q in range(4):
-                queue.dma_start(out=planes[32 * q:32 * q + 4, i, :].bitcast(I32), in_=rows[4 * q:4 * q + 4, :])
-            return planes[:, i, :]
+            for q in (2 * g, 2 * g + 1):
+                nc.sync.dma_start(out=planes[32 * q:32 * q + 4, i, :].bitcast(I32), in_=rows[4 * q:4 * q + 4, :])
 
         x_raw = load_rows("x_raw", x)
-        w1 = (load_words("w1", w1_words), load_scales(nc.scalar, 0, w1_scales))
-        w2 = (load_words("w2", w2_words), load_scales(nc.gpsimd, 1, w2_scales))
+        w1 = (load_words("w1", w1_words), planes[:, 0, :])
+        w2 = (load_words("w2", w2_words), planes[:, 1, :])
+        load_scales(0, w1_scales, 0)
+        load_scales(1, w2_scales, 0)
         dy_raw = load_rows("dy_raw", dy)
-        wo = (load_words("wo", wo_words), load_scales(nc.sync, 2, wo_scales))
+        load_scales(0, w1_scales, 1)
+        load_scales(1, w2_scales, 1)
+        wo = (load_words("wo", wo_words), planes[:, 2, :])
+        load_scales(2, wo_scales, 0)
+        load_scales(2, wo_scales, 1)
         th_sb = sb.tile([P, G, M // P], F32, name="th_sb")
         with nc.allow_non_contiguous_dma(reason="one threshold a partition"):
             nc.sync.dma_start(out=th_sb[:], in_=th.rearrange("g (h p) o -> p g (h o)", p=P))
@@ -147,11 +152,11 @@ def tile_rows_bmagnitude_kernel(tc, x, w1_words, w1_scales, w2_words, w2_scales,
         root(0)
         magnitude(nc.gpsimd, 0, 0, N)
         step_e(0)
-        nc.vector.tensor_scalar(out=neg_th[:], in0=th_sb[:], scalar1=-1.0, scalar2=None, op0=ALU.mult)
         step_f(0)
         squares(2)
         product(zc[2], wo, dyq, 2)
         add(2)
+        nc.vector.tensor_scalar(out=neg_th[:], in0=th_sb[:], scalar1=-1.0, scalar2=None, op0=ALU.mult)
         squares(3)
         product(zc[3], wo, dyq, 3)
         add(3)
@@ -179,5 +184,7 @@ def tile_rows_bmagnitude_kernel(tc, x, w1_words, w1_scales, w2_words, w2_scales,
             for t in (pair, pair + 1):
                 nc.vector.tensor_tensor(out=m[t][:], in0=k[t][:], in1=pre[t][:], op=ALU.mult)
             for t in (pair, pair + 1):
-                nc.vector.tensor_tensor(out=res[t][:], in0=old_sb[:, (M // P) * group(t) + half(t), :], in1=m[t][:], op=ALU.subtract)
-                nc.sync.dma_start(out=out[group(t), P * half(t):P * (half(t) + 1), :], in_=res[t][:])
+                cuts = (0, N // 2, N) if t == TILES - 1 else (0, N)
+                for lo, hi in zip(cuts, cuts[1:]):
+                    nc.vector.tensor_tensor(out=res[t][:, lo:hi], in0=old_sb[:, t, lo:hi], in1=m[t][:, lo:hi], op=ALU.subtract)
+                    nc.sync.dma_start(out=out[group(t), P * half(t):P * (half(t) + 1), lo:hi], in_=res[t][:, lo:hi])

from contextlib import ExitStack

import concourse.mybir as mybir

G, D, M, N = 2, 256, 256, 512
FLOPS = 3 * 2 * G * D * M * N

F32 = mybir.dt.float32
BF16 = mybir.dt.bfloat16
I32 = mybir.dt.int32
U32 = mybir.dt.uint32
U8 = mybir.dt.uint8
FP8X4 = mybir.dt.float8_e4m3fn_x4
FP4X4 = mybir.dt.float4_e2m1fn_x4
ACT = mybir.ActivationFunctionType
ALU = mybir.AluOpType

P = 128
PACK = 4
ROWS = D // PACK
TILES = G * M // P
FLOOR = 0.05
X_SPLIT = 336
MG_SPLIT = 256


def tile_rows_bmagnitude_kernel(tc, x, w1_words, w1_scales, w2_words, w2_scales, th, wo_words, wo_scales, dy, old, out):
    nc = tc.nc
    with ExitStack() as ctx:
        sb = ctx.enter_context(tc.tile_pool(name="sb", bufs=1))
        ps = ctx.enter_context(tc.psum_pool(name="ps", bufs=1))
        ctx.enter_context(tc.manual_schedule())

        def group(t):
            return t // 2

        def half(t):
            return t % 2

        def load_rows(name, src):
            raw = sb.tile([P, PACK, N], F32, name=name)
            nc.sync.dma_start(out=raw[:], in_=src.rearrange("g (p j) n -> (g p) j n", j=PACK))
            return raw

        def load_words(name, words):
            w = sb.tile([P, 2 * M], U8, name=name, align_bytes=64)
            nc.sync.dma_start(out=w[:].bitcast(I32), in_=words.rearrange("g p b -> (g p) b").bitcast(I32))
            return w

        planes = sb.tile([P, 3, M], U8, name="planes", align_bytes=64)
        nc.vector.memset(planes[:].rearrange("p i m -> p (i m)").bitcast(I32), 0)

        def load_scales(i, scales, g):
            rows = scales.rearrange("g f m -> (g f) m").bitcast(I32)
            for q in (2 * g, 2 * g + 1):
                nc.sync.dma_start(out=planes[32 * q:32 * q + 4, i, :].bitcast(I32), in_=rows[4 * q:4 * q + 4, :])

        x_raw = load_rows("x_raw", x)
        w1 = (load_words("w1", w1_words), planes[:, 0, :])
        w2 = (load_words("w2", w2_words), planes[:, 1, :])
        load_scales(0, w1_scales, 0)
        load_scales(1, w2_scales, 0)
        dy_raw = load_rows("dy_raw", dy)
        load_scales(0, w1_scales, 1)
        load_scales(1, w2_scales, 1)
        wo = (load_words("wo", wo_words), planes[:, 2, :])
        load_scales(2, wo_scales, 0)
        load_scales(2, wo_scales, 1)
        th_sb = sb.tile([P, G, M // P], F32, name="th_sb")
        with nc.allow_non_contiguous_dma(reason="one threshold a partition"):
            nc.sync.dma_start(out=th_sb[:], in_=th.rearrange("g (h p) o -> p g (h o)", p=P))
        old_sb = sb.tile([P, G * (M // P), N], F32, name="old_sb")
        nc.sync.dma_start(out=old_sb[:], in_=old.rearrange("g (h p) n -> p (g h) n", p=P))

        warm = sb.tile([P, 8], F32, name="warm")
        nc.vector.memset(warm[:, 0:1], 1.0)
        warm_out = sb.tile([P, 8], F32, name="warm_out")
        nc.scalar.activation(out=warm_out[:, 0:1], in_=warm[:, 0:1], func=ACT.Abs_reciprocal_sqrt)

        def interleave(copy, grouped, raw, lo, hi):
            copy(out=grouped[:, lo:hi, :].rearrange("p (c i) j -> p c j i", i=4),
                 in_=raw[:, :, lo:hi].rearrange("p j (c i) -> p c j i", i=4))

        def quantize(name, grouped):
            codes = sb.tile([P, N], U32, name=name + "_codes", align_bytes=64)
            scales = sb.tile([P, N], U8, name=name + "_scales", align_bytes=64)
            nc.vector.quantize_mx(out=codes[:].bitcast(FP8X4), scales=scales[:], in_=grouped[:].rearrange("p n j -> p (n j)"))
            return codes, scales

        def product(bank, weights, moving, t):
            rows = slice(ROWS * group(t), ROWS * (group(t) + 1))
            w, ws = weights
            codes, scales = moving
            nc.tensor.matmul_mx(
                out=bank[:],
                lhsT=w[rows, 2 * P * half(t):2 * P * (half(t) + 1)].bitcast(FP4X4),
                lhsT_scale=ws[rows, P * half(t):P * (half(t) + 1)],
                rhs=codes[rows, :].bitcast(FP8X4),
                rhs_scale=scales[rows, :],
                start=True,
                stop=True,
            )

        def tiles(name):
            return [sb.tile([P, N], F32, name="%s%d" % (name, t)) for t in range(TILES)]

        x_grouped = sb.tile([P, N, PACK], BF16, name="x_grouped", align_bytes=64)
        interleave(nc.vector.tensor_copy, x_grouped, x_raw, 0, X_SPLIT)
        interleave(nc.scalar.copy, x_grouped, x_raw, X_SPLIT, N)
        xq = quantize("x", x_grouped)

        z1 = [ps.tile([P, N], F32, name="z1_%d" % t) for t in range(TILES)]
        zc = [ps.tile([P, N], F32, name="zc_%d" % t) for t in range(TILES)]
        for t in range(TILES):
            product(z1[t], w1, xq, t)
            product(zc[t], w2, xq, t)

        sq1, sq2, ss, rs, mg = tiles("sq1_"), tiles("sq2_"), tiles("ss"), tiles("rs"), tiles("mg")
        cosine, pre, sig = tiles("cosine"), tiles("pre"), tiles("sig")
        h, k, m, res = tiles("h"), tiles("k"), tiles("m"), tiles("res")

        def squares(t):
            nc.scalar.activation(out=sq1[t][:], in_=z1[t][:], func=ACT.Square)
            nc.scalar.activation(out=sq2[t][:], in_=zc[t][:], func=ACT.Square)

        def add(t):
            nc.vector.scalar_tensor_tensor(out=ss[t][:], in0=sq1[t][:], scalar=FLOOR, in1=sq2[t][:], op0=ALU.add, op1=ALU.add)

        def root(t):
            nc.scalar.activation(out=rs[t][:], in_=ss[t][:], func=ACT.Abs_reciprocal_sqrt)

        def magnitude(eng, t, lo, hi):
            eng.tensor_tensor(out=mg[t][:, lo:hi], in0=ss[t][:, lo:hi], in1=rs[t][:, lo:hi], op=ALU.mult)

        def step_e(t):
            nc.vector.tensor_tensor(out=cosine[t][:], in0=rs[t][:], in1=z1[t][:], op=ALU.mult)

        def step_f(t):
            nc.vector.tensor_tensor(out=pre[t][:], in0=cosine[t][:], in1=zc[t][:], op=ALU.mult)

        dy_grouped = sb.tile([P, N, PACK], BF16, name="dy_grouped", align_bytes=64)
        neg_th = sb.tile([P, G, M // P], F32, name="neg_th")

        squares(0)
        interleave(nc.vector.tensor_copy, dy_grouped, dy_raw, 0, N)
        add(0)
        squares(1)
        dyq = quantize("dy", dy_grouped)
        product(zc[0], wo, dyq, 0)
        product(zc[1], wo, dyq, 1)
        add(1)
        root(0)
        magnitude(nc.gpsimd, 0, 0, N)
        step_e(0)
        step_f(0)
        squares(2)
        product(zc[2], wo, dyq, 2)
        add(2)
        nc.vector.tensor_scalar(out=neg_th[:], in0=th_sb[:], scalar1=-1.0, scalar2=None, op0=ALU.mult)
        squares(3)
        product(zc[3], wo, dyq, 3)
        add(3)
        for t in range(1, TILES):
            root(t)
        magnitude(nc.gpsimd, 1, 0, N)
        magnitude(nc.gpsimd, 2, 0, N)
        magnitude(nc.gpsimd, 3, 0, MG_SPLIT)
        step_e(1)
        step_e(2)
        step_f(1)
        step_e(3)
        step_f(2)
        step_f(3)
        magnitude(nc.vector, 3, MG_SPLIT, N)

        for t in range(TILES):
            nc.scalar.activation(out=sig[t][:], in_=mg[t][:], func=ACT.Sigmoid, bias=neg_th[:, group(t), half(t):half(t) + 1])

        for pair in range(0, TILES, 2):
            for t in (pair, pair + 1):
                nc.vector.scalar_tensor_tensor(out=h[t][:], in0=sig[t][:], scalar=1.0, in1=mg[t][:], op0=ALU.subtract, op1=ALU.mult)
            for t in (pair, pair + 1):
                nc.vector.scalar_tensor_tensor(out=k[t][:], in0=h[t][:], scalar=1.0, in1=sig[t][:], op0=ALU.subtract, op1=ALU.mult)
            for t in (pair, pair + 1):
                nc.vector.tensor_tensor(out=m[t][:], in0=k[t][:], in1=pre[t][:], op=ALU.mult)
            for t in (pair, pair + 1):
                cuts = (0, N // 2, N) if t == TILES - 1 else (0, N)
                for lo, hi in zip(cuts, cuts[1:]):
                    nc.vector.tensor_tensor(out=res[t][:, lo:hi], in0=old_sb[:, t, lo:hi], in1=m[t][:, lo:hi], op=ALU.subtract)
                    nc.sync.dma_start(out=out[group(t), P * half(t):P * (half(t) + 1), lo:hi], in_=res[t][:, lo:hi])
